import numpy as np, ml_dtypes
CORES = [3,7,11,15,131,135,139,143]
N = 8
BF = ml_dtypes.bfloat16
W, V, Q, S, RO = 2048, 256, 4, 5, 3
RK = np.arange(N)[:, None, None]; GR = np.arange(8)[None, :, None]; VE = np.arange(V)[None, None, :]
def unfold(a, m):
    return np.ascontiguousarray(a.reshape(N, 8, 16, m).transpose(0, 1, 3, 2))
def fold(a):
    return np.ascontiguousarray(a.transpose(0, 1, 3, 2)).reshape(N, 128, -1)
def pack(T, U, P, x):
    return {"tx": fold(T).astype(np.float32).astype(BF), "pu": fold(U).astype(np.int32), "p0": fold(P).astype(np.int32), "x0": fold(x).astype(np.float32).astype(BF)}
def pair(rng, P):
    m = rng.integers(0, 17, (N, 8, V // 2, 1))
    P[:, :, 1::2] = np.where(np.arange(16) < m, P[:, :, 0::2], P[:, :, 1::2])
    return P
def parts(rng):
    T = rng.integers(0, 128, (N, 8, W, 16)); U = rng.integers(0, W, (N, 8, W, 16))
    U = np.where(rng.random((N, 8, W, 1)) < 0.25, U[..., :1], U)
    P = rng.integers(0, W, (N, 8, V, 16))
    for k in range(1, 16):
        nxt = U[RK, GR, P[..., k - 1], rng.integers(0, 16, (N, 8, V))]
        P[..., k] = np.where(rng.random((N, 8, V)) < 0.5, nxt, P[..., k])
    P = pair(rng, P)
    near = np.clip(T[RK, GR, P[..., 15]] + rng.integers(-20, 21, (N, 8, V, 16)), 0, 127)
    x = np.where(rng.random((N, 8, V, 1)) < 0.5, near, rng.integers(0, 128, (N, 8, V, 16)))
    return T, U, P, x
def setup_inputs(rng):
    return pack(*parts(rng))
def setup_inputs_ties(rng):
    T, U, P, x = parts(rng)
    few = rng.integers(0, 128, (N, 8, 6, 16)); few[:, :, 0] = 0; few[:, :, 1] = 127
    T = few[RK, GR, rng.integers(0, 6, (N, 8, W))]; x = few[RK, GR, rng.integers(0, 6, (N, 8, V))]
    return pack(T, U, P, x)
def setup_inputs_cuts(rng):
    T, U, P, x = parts(rng); h = W // 2; s = V // 4
    for g in range(8):
        o = rng.permutation(W); P[:, g] = o[h + P[:, g] % h]
        for j in range(s):
            m = (1, Q - 1, Q, N)[j if j < 4 else int(rng.integers(0, 4))]
            nm = o[s + np.arange(N)]; nm[rng.permutation(N)[:m]] = o[j]
            P[:, g, 2 * j + 1] = P[:, g, 2 * j]; P[:, g, 2 * j:2 * j + 2, 15] = nm[:, None]
    return pack(T, U, P, x)
def setup_inputs_crowd(rng):
    T, U, P, x = parts(rng); h = V // 2; r = np.arange(N)[:, None]; j = np.arange(h)[None, :]
    for g in (0, 1, 2, 3, 4, 5, 7):
        o = rng.permutation(W); nm = np.repeat(o[1:N + 1, None], V, axis=1); n = N + 1
        if g in (0, 7):
            if g == 7: o = np.concatenate([np.array([W - 1]), rng.permutation(W - 1)])
            nm = np.stack([rng.permutation(o[i * V:(i + 1) * V]) for i in np.minimum(rng.permutation(N) // Q, N // Q - 1)]); n = (N // Q) * V
        elif g in (1, 4):
            o = 1 + rng.permutation(W - 1); n = ((N - 1) // (Q - 1) + 1) * h
            nm = o[(rng.permutation(N) // (Q - 1))[:, None] * h + np.arange(V)[None, :] // 2]
        elif g == 2: nm[rng.permutation(N)[:Q]] = o[0]
        elif g == 5:
            s = int(rng.integers(0, N - Q + 1)); nm[s:s + Q - 1, :192] = o[0]; nm = nm[:, rng.permutation(V)]
        else: o = np.arange(W)[::-1]; n = 512
        a, b = o[:n], o[n:]
        T[:, g] = T[:, g] >> 2; x[:, g] = x[:, g] >> 2; T[:, g, a] = T[:, g, a] + 96
        P[:, g] = b[P[:, g] % len(b)]; U[:, g] = b[U[:, g] % len(b)]; P[:, g, 1::2] = np.array(P[:, g, 0::2])
        if g == 3:
            m = rng.integers(1, 15, (N, h)); c = W - 512 + 4 * rng.integers(0, 128, (N, h))
            P[r, g, 2 * j, m] = c; P[r, g, 2 * j + 1, m] = c + 1
        else: P[:, g, :, 15] = nm
        if g in (0, 7): P[:, g, :, 14] = np.array(P[:1, g, :, 14]); U[:, g] = np.array(U[:1, g, :, :1])
    return pack(T, U, P, x)
def setup_inputs_few(rng):
    T, U, P, x = parts(rng)
    for g in (0, 2, 4, 6):
        a = np.concatenate([np.array([0, W - 1]), rng.integers(0, W, 10)]); P[:, g] = a[P[:, g] % 12]
        if g in (0, 4): U[:, g] = a[U[:, g] % 12]
    P[:, 2] = np.array(P[:, 2, :, :1]); U[:, 4, ::2] = rng.integers(0, W, (N, W // 2, 16)); U[:, 6] = np.arange(W)[:, None]
    return pack(T, U, P, x)
def setup_inputs_spread(rng):
    T = np.minimum((np.exp2(7 * rng.random((N, 8, W, 1))) * rng.random((N, 8, W, 16))).astype(np.int64), 127)
    x = np.minimum((np.exp2(7 * rng.random((N, 8, V, 1))) * rng.random((N, 8, V, 16))).astype(np.int64), 127)
    U = np.minimum((W * rng.random((N, 8, W, 16)) ** 2).astype(np.int64), W - 1)
    P = np.minimum((W * rng.random((N, 8, V, 16)) ** 3).astype(np.int64), W - 1)
    return pack(T, U, pair(rng, P), x)
def check_inputs(d):
    bad = []
    for k, hi in (("tx", 127), ("pu", W - 1), ("p0", W - 1), ("x0", 127)):
        a = np.asarray(d[k]).astype(np.float64)
        if not (np.all(a >= 0) and np.all(a <= hi)): bad.append("range of " + k)
        elif np.any(np.floor(a) != a): bad.append("whole numbers of " + k)
    return bad
def reference(tx, pu, p0, x0):
    T = unfold(tx.astype(np.float32).astype(np.int32), W); U = unfold(pu.astype(np.int64), W)
    P = unfold(p0.astype(np.int64), V); x = unfold(x0.astype(np.float32).astype(np.int32), V)
    row = np.arange(16); cut = np.zeros((8, W), bool); R4 = RK[..., None]; G4 = GR[..., None]
    for rnd in range(RO):
        d = np.add.reduce(np.abs(T[R4, G4, P] - x[:, :, :, None, :]), axis=4)
        differ = P != P[:, :, np.arange(V) ^ 1]
        q = np.where(np.any(differ, axis=3), np.argmax(differ, axis=3), 15)
        f = np.argmax(np.where(row >= np.maximum(q, 1)[..., None], d, -1), axis=3)
        old = cut[G4, P] & (row >= 1)
        k = np.where(np.any(old, axis=3), np.argmax(old, axis=3), f)
        charged = np.zeros((N, 8, W), bool); charged[RK, GR, P[RK, GR, VE, f]] = True
        cut = cut | (np.add.reduce(charged.astype(np.int64), axis=0) >= Q)
        T[:, cut] = 256
        pup = U[RK, GR, P[RK, GR, VE, k - 1]]
        e = np.add.reduce(np.abs(T[R4, G4, pup] - x[:, :, :, None, :]), axis=4)
        b = np.argmin(e, axis=3); best = pup[RK, GR, VE, b]
        take = e[RK, GR, VE, b] < d[RK, GR, VE, k]
        P[RK, GR, VE, k] = np.where(take, best, P[RK, GR, VE, k])
        x = np.where(take[..., None], (x + T[RK, GR, best]) >> 1, x)
        if rnd + 1 < RO: P = np.roll(P, S, axis=0); x = np.roll(x, S, axis=0)
    return {"yp": fold(P).astype(np.float32), "yx": fold(x).astype(np.float32).astype(BF), "yc": np.repeat(cut[None], N, axis=0).astype(np.float32)}

@@ -1,0 +1,457 @@
+from concourse.bass import DstId, RemoteDMATransfer
+from concourse.mybir import dt, AluOpType as OP, ActivationFunctionType as AF
+
+NR = 3
+STEP = 5
+NG = 8
+BIG = 262144.0
+
+F4, BF, HF, I4, U2 = "float32", "bfloat16", "float16", "int32", "uint16"
+SCRATCH = {}
+for _n, _w, _d in (
+        ("TXR", 2048, BF), ("TX", 2304, BF), ("PU", 2048, I4), ("P0R", 256, I4), ("X0R", 256, BF),
+        ("XR", 1024, BF), ("DF", 4096, BF), ("AD", 4096, BF), ("OU", 2048, BF), ("OV", 2048, BF),
+        ("PI", 8, I4), ("PF", 12, F4), ("IF", 144, F4), ("MU", 128, F4), ("MG", 128, F4), ("FS", 144, BF), ("ID", 128, BF), ("SW", 512, HF),
+        ("ONB", 128, BF), ("ONF", 256, F4), ("NEGC", 128, F4), ("BGC", 256, F4), ("REP", 2048, BF), ("BD", 128, BF), ("H16", 16, F4),
+        ("IU", 128, BF), ("IV", 128, BF), ("BDM", 128, F4), ("KREV", 256, F4), ("KRV0", 128, F4), ("NEGM", 128, F4), ("RES", 256, F4),
+        ("RES1", 256, F4), ("RESB", 256, F4), ("BIGK", 256, F4), ("BASE", 16, F4), ("BKA", 256, F4), ("BKB", 256, F4),
+        ("A16", 256, HF), ("FM", 256, F4), ("RR", 256, F4), ("D1", 256, F4), ("LT", 256, F4), ("PAYI", 16, I4), ("UVI", 32, I4), ("UVF", 32, F4),
+        ("TEI", 16, I4), ("TEO", 16, U2), ("PKI", 16, I4), ("PK", 16, F4), ("DKM", 16, F4), ("DKI", 16, I4), ("DKJ", 16, I4), ("KB", 256, F4),
+        ("OH", 256, F4), ("PZ", 256, F4), ("THA", 128, F4), ("THB", 256, F4), ("T1", 256, F4), ("PDO", 256, U2), ("CUT", 128, BF),
+        ("CAC", 128, F4), ("CA2", 128, F4), ("BE", 16, F4), ("TK", 16, F4), ("O1", 16, F4), ("O2", 16, F4), ("OF", 16, F4), ("OFO", 16, U2),
+        ("N1", 16, F4), ("N2", 16, F4), ("SU", 256, F4), ("EQ", 128, F4), ("PRE", 128, F4), ("PM", 128, F4), ("TA", 256, F4), ("TB", 256, F4),
+        ("YPA", 256, F4), ("YPB", 256, F4), ("YXB", 256, BF)):
+    SCRATCH[_n] = ("sbuf", [128, _w], _d)
+SCRATCH["XQ"] = ("sbuf", [128, 16, 4, 16], BF)
+for _n, _c, _d in (("C16", 16, HF), ("PNH", 16, HF), ("PFL", 16, F4), ("KFW", 8, BF)):
+    SCRATCH[_n] = ("sbuf", [128, _c, 16], _d)
+for _n, _c in (("dps", 16), ("eps", 16), ("t0", 32), ("t1", 32)):
+    SCRATCH[_n] = ("psum", [128, _c, 16], F4)
+for _n in ("mps", "kps", "t2", "t3"):
+    SCRATCH[_n] = ("psum", [128, 512], F4)
+for _r in range(NR):
+    SCRATCH["Y%d" % _r] = ("sbuf", [128, 256], BF)
+    SCRATCH["YS%d" % (_r + 1)] = ("sbuf", [128, 256], BF)
+    for _s in ("", "S") if _r else ("",):
+        SCRATCH["PO%s%d" % (_s, _r)] = ("sbuf", [128, 256], U2)
+        SCRATCH["KM%s%d" % (_s, _r)] = ("sbuf", [128, 8, 16], BF)
+        SCRATCH["PA%s%d" % (_s, _r)] = ("sbuf", [128, 256], F4)
+    SCRATCH["MK%d" % _r] = ("sbuf", [128, 1024], BF)
+    SCRATCH["MS%d" % _r] = ("sbuf", [128, 128], BF)
+PSUM = [n for n in SCRATCH if SCRATCH[n][0] == "psum"]
+
+LOADS = ["lp0", "lx0", "ltx0", "ltx1", "ltx2", "ltx3", "lpu0", "lpu1"]
+SEMAPHORES = (["qv", "qs", "qp", "qg", "loc", "oyp", "oyx", "oyc"] + LOADS + ["mk%d_%d" % (r, j) for r in range(NR) for j in range(NG)]
+              + ["%s_%d" % (n, r) for r in range(1, NR) for n in ("ry", "rp", "rk", "ra")])
+
+
+def rank_program(g, core, T, topo):
+    rank = T.rank_of(core)
+    if rank is None:
+        return
+    Q = {"V": g.vector, "S": g.scalar, "P": g.tensor, "G": g, "Y": g.sync}
+    SEM = {"V": "qv", "S": "qs", "P": "qp", "G": "qg"}
+    cnt = {"V": 0, "S": 0, "P": 0, "G": 0}
+    known = {q: {} for q in Q}
+    acc = {}
+    sent = [0]
+
+    def A(n, lo=0, hi=None, st=1):
+        hi = SCRATCH[n][1][1] if hi is None else hi
+        return (T[n][:, lo:hi] if st == 1 else T[n][:, lo:hi:st], n, lo, hi)
+
+    def B(ap, n, lo, hi):
+        return (ap, n, lo, hi)
+
+    def need(q, ins, outs):
+        w = {}
+        for isw, ops in ((False, ins), (True, outs)):
+            for (_, n, lo, hi) in ops:
+                for (l2, h2, w2, q2, s2, v2) in acc.get(n, ()):
+                    ps = n in PSUM
+                    if ps and q2 == q and q == "P":
+                        continue
+                    hit = ps and q2 != q
+                    hit = hit or ((isw or w2) and lo < h2 and l2 < hi)
+                    if hit and known[q].get(s2, 0) < v2:
+                        w[s2] = max(w.get(s2, 0), v2)
+        for s in sorted(w):
+            Q[q].wait_ge(T.sem[s], w[s])
+            known[q][s] = w[s]
+
+    def note(q, s, v, ins, outs):
+        for (_, n, lo, hi) in outs:
+            acc[n] = [e for e in acc.get(n, []) if (e[3] == q or n not in PSUM) and not (lo <= e[0] and e[1] <= hi)]
+            acc[n].append((lo, hi, True, q, s, v))
+        for (_, n, lo, hi) in ins:
+            acc.setdefault(n, []).append((lo, hi, False, q, s, v))
+
+    def do(q, f, outs, ins):
+        need(q, ins, outs)
+        f().then_inc(T.sem[SEM[q]], 1)
+        cnt[q] += 1
+        note(q, SEM[q], cnt[q], ins, outs)
+
+    def cp(o, i):
+        do("V", lambda: g.vector.tensor_copy(o[0], i[0]), [o], [i])
+
+    def tt(o, a, b, op):
+        do("V", lambda: g.vector.tensor_tensor(o[0], a[0], b[0], op), [o], [a, b])
+
+    def ts(o, a, s1, op0, s2=None, op1=None):
+        extra = [s for s in (s1, s2) if isinstance(s, tuple)]
+        v1 = s1[0] if isinstance(s1, tuple) else s1
+        v2 = s2[0] if isinstance(s2, tuple) else s2
+        if op1 is None:
+            do("V", lambda: g.vector.tensor_scalar(o[0], a[0], v1, None, op0), [o], [a] + extra)
+        else:
+            do("V", lambda: g.vector.tensor_scalar(o[0], a[0], v1, v2, op0, op1), [o], [a] + extra)
+
+    def scan(o, d0, d1, op0, op1):
+        do("V", lambda: g.vector.tensor_tensor_scan(o[0], d0[0], d1[0], 0.0, op0, op1), [o], [d0, d1])
+
+    def t32(o, i):
+        do("V", lambda: g.vector.transpose(o[0], i[0]), [o], [i])
+
+    def gat(o, win, off, in1=None, op=None):
+        ap = win[0].indirect(off[0])
+        if in1 is None:
+            do("V", lambda: g.vector.tensor_copy(o[0], ap), [o], [win, off])
+        else:
+            do("V", lambda: g.vector.tensor_tensor(o[0], ap, in1[0], op), [o], [win, off, in1])
+
+    def act(o, i, func=AF.Identity, scale=1.0, bias=0.0):
+        do("S", lambda: g.scalar.activation(o[0], i[0], func, bias=bias, scale=scale), [o], [i])
+
+    def mm(o, l, r, start, stop):
+        do("P", lambda: g.tensor.matmul(o[0], l[0], r[0], start, stop), [o], [l, r])
+
+    def iota(o, pat, base, cm):
+        if SCRATCH[o[1]][2] == I4:
+            do("G", lambda: g.iota(o[0], pat, base, cm), [o], [])
+        else:
+            do("G", lambda: g.iota(o[0], pat, base, cm, allow_small_or_imprecise_dtypes=True), [o], [])
+
+    def keep(o, i, pat, cmp, fill, base, cm):
+        do("G", lambda: g.affine_select(o[0], i[0], pat, cmp, fill, base, cm), [o], [i])
+
+    def load(q, o, src, sem):
+        Q[q].dma_start(o[0], src).then_inc(T.sem[sem], 16)
+        note(q, sem, 16, [], [o])
+
+    def store(q, dst, i, sem):
+        need(q, [i], [])
+        Q[q].dma_start(dst, i[0]).then_inc(T.sem[sem], 16)
+
+    def engs(src, dsts):
+        e = [x for x in topo.engines(src, dsts[0]) if all(x in topo.engines(src, d) for d in dsts)]
+        n = 1
+        while 2 * n <= min(len(e), 8):
+            n *= 2
+        return e[:n]
+
+    def send(i, dsts, out, sem):
+        need("G", [i], [])
+        e = engs(core, dsts)
+        m = 0
+        for x in e:
+            m |= 1 << x
+        ids = []
+        for d in dsts:
+            rid, pid = topo.addr(d, core)
+            ids.append(DstId(rid=rid, pnc=pid))
+        g.remote_dma_fused([RemoteDMATransfer(dst_ids=ids, dma_engine_mask=m, remote_sem=T.sem[sem], srcs=[i[0]], dsts=[out for d in dsts])],
+                           local_sem=T.sem.loc)
+        sent[0] += len(e)
+
+    def land(o, sem, src, dsts):
+        note("R", sem, len(engs(src, dsts)), [], [o])
+
+    nxt = T.cores[(rank + STEP) % NG]
+    prv = T.cores[(rank - STEP) % NG]
+
+    def rest(j):
+        return [c for c in T.cores if c != T.cores[j]]
+
+    load("Y", A("P0R"), T.p0[:], "lp0")
+    load("S", A("X0R"), T.x0[:], "lx0")
+    for j in range(4):
+        load("Y" if j % 2 == 0 else "S", A("TXR", 512 * j, 512 * j + 512), T.tx[:, 512 * j:512 * j + 512], "ltx%d" % j)
+    for j in range(2):
+        load("Y", A("PU", 1024 * j, 1024 * j + 1024), T.pu[:, 1024 * j:1024 * j + 1024], "lpu%d" % j)
+
+    def col(j):
+        return A("PF", j, j + 1)
+
+    CK = [[0, 16], [1, 16]]
+    iota(A("PI", 0, 1), [[0, 1]], 0, 1)
+    iota(A("IF"), [[1, 144]], 0, 0)
+    iota(A("ONB"), [[0, 128]], 1, 0)
+    keep(A("ID"), A("ONB"), [[-1, 128]], OP.is_equal, 0.0, 0, 1)
+    iota(A("KREV"), [[0, 16], [-1, 16]], 15, 0)
+    keep(A("KRV0"), A("KREV", 0, 128), [[0, 8], [1, 16]], OP.is_gt, -BIG, 0, 0)
+    iota(A("ONF"), [[0, 256]], 1, 0)
+    keep(A("RES1"), A("ONF"), CK, OP.is_equal, 0.0, 0, 0)
+    iota(A("NEGC"), [[0, 128]], -262144, 0)
+    keep(A("NEGM"), A("NEGC"), [[0, 8], [-1, 16]], OP.is_ge, 0.0, 14, 0)
+    keep(A("RES"), A("ONF"), CK, OP.is_gt, 0.0, 0, 0)
+    for r in range(NR):
+        iota(A("PA0" if r == 0 else "PAS%d" % r, 0, 1), [[0, 1]], 1, 0)
+    iota(A("MU"), [[0, 8], [1, 16]], 0, 0)
+    iota(A("MG"), [[1, 8], [0, 16]], 0, 0)
+    iota(A("IV"), [[1, 128]], 0, 0)
+    iota(A("KFW"), [[0, 8], [1, 16]], 0, 0)
+    iota(A("BASE"), [[16, 16]], 2048, 0)
+    iota(A("BKA"), [[0, 256]], 0, 0)
+    iota(A("BKB"), [[0, 256]], 0, 0)
+    iota(A("BGC"), [[0, 16], [-1, 16]], 262144 + 15, 0)
+    keep(A("BIGK"), A("BGC"), CK, OP.is_gt, 0.0, 0, 0)
+    act(A("RESB"), A("RES1"), scale=1048576.0)
+    AND, SHR = OP.bitwise_and, OP.arith_shift_right
+    ts(A("PI", 1, 2), A("PI", 0, 1), 15, AND)
+    ts(A("PI", 2, 3), A("PI", 0, 1), 4, SHR)
+    ts(A("PI", 3, 4), A("PI", 0, 1), 4, SHR, 1, AND)
+    ts(A("PI", 4, 5), A("PI", 0, 1), 112, AND)
+    cp(A("PF", 0, 5), A("PI", 0, 5))
+    ts(A("PF", 6, 7), A("PF", 3, 4), -1000.0, OP.mult)
+    ts(A("PF", 7, 8), A("PF", 3, 4), 1000.0, OP.mult, -1000.0, OP.add)
+    tt(A("PF", 8, 9), A("PF", 6, 7), A("PF", 0, 1), OP.add)
+    tt(A("PF", 9, 10), A("PF", 7, 8), A("PF", 0, 1), OP.add)
+    ts(A("PF", 10, 11), A("PF", 4, 5), 15.0, OP.add)
+    for x in range(2):
+        for y in range(2):
+            j = 2 * x + y
+            ts(A("SW", 128 * j, 128 * j + 128), A("IF", 0, 128), float(16 * (y - x)), OP.subtract, col(8 + x), OP.is_equal)
+
+    def swap(dst, src):
+        for x in range(2):
+            for y in range(2):
+                j = 2 * x + y
+                mm(B(T[dst][:, x:16:2, :], dst, 0, 16), A("SW", 128 * j, 128 * j + 128), B(T[src][:, y:16:2, :], src, 0, 16), y == 0, y == 1)
+
+    def offs(o, sn):
+        for h in range(4):
+            cp(A(o, 64 * h, 64 * h + 64), B(T[sn][:, 0:16, 4 * h:4 * h + 4], sn, 0, 16))
+
+    for h in range(2):
+        cp(A("A16", 128 * h, 128 * h + 128), A("P0R", h, 256, 2))
+    t32(A("C16"), A("A16"))
+    swap("t1", "C16")
+    T1D = B(T.t1[:, 0:16, :], "t1", 0, 16)
+    offs("PO0", "t1")
+    cp(A("PFL"), T1D)
+    for h in range(2):
+        ts(A("Y0", 128 * h, 128 * h + 128), A("X0R", h, 256, 2), -1.0, OP.mult, 256.0, OP.add)
+    ts(A("FS"), A("IF"), col(10), OP.is_equal, 32.0, OP.mult)
+
+    def pay0():
+        act(A("TA"), A("PFL"), scale=2.0 ** -11, bias=1.0)
+        act(A("TB"), A("PFL"), scale=2.0 ** -22)
+
+    def pay1(pa):
+        tt(A(pa, 1, 256), A("TA", 1, 256), A("TB", 0, 255), OP.add)
+
+    def pens(km):
+        P = T.PFL
+        tt(A("EQ"), B(P[:, 0:8, :], "PFL", 0, 8), B(P[:, 8:16, :], "PFL", 8, 16), OP.is_equal)
+        scan(A("PRE"), A("RES1", 0, 128), A("EQ"), OP.max, OP.min)
+        tt(A("PM"), A("PRE"), A("NEGM"), OP.mult)
+        tt(A(km), A("PM"), A("KRV0"), OP.add)
+
+    for j in range(4):
+        o, i = A("TX", 512 * j, 512 * j + 512), A("TXR", 512 * j, 512 * j + 512)
+        if j % 2 == 0:
+            ts(o, i, -1.0, OP.mult, 256.0, OP.add)
+        else:
+            act(o, i, scale=-1.0, bias=256.0)
+    WIN = A("TX", 0, 2048)
+
+    def tables():
+        ts(A("BDM"), A("MG"), col(2), OP.is_equal)
+        ts(A("T1", 0, 128), A("MU"), 1.0, OP.add)
+        tt(A("T1", 128, 256), A("T1", 0, 128), A("BDM"), OP.mult)
+        ts(A("IU"), A("T1", 128, 256), -1.0, OP.add)
+
+    def tables2():
+        ts(A("BD"), A("BDM"), -256.0, OP.mult)
+        ts(A("H16"), A("IF", 0, 16), col(1), OP.is_equal)
+        for u in range(16):
+            ts(A("REP", 128 * u, 128 * u + 128), A("BD"), A("H16", u, u + 1), OP.mult)
+        ts(A("O1"), A("BASE"), col(1), OP.add)
+        cp(A("BASE"), A("O1"))
+
+    def spread(yn, c0, c1, q):
+        f = cp if q == "V" else (lambda o, i: act(o, i, AF.Copy))
+        X, y = T.XQ, A(yn, 16 * c0, 16 * c1)
+        f(B(X[:, c0:c1, 0, :], "XQ", 4 * c0, 4 * c0 + 1), y)
+        f(B(X[:, c0:c1, 1, :], "XQ", 4 * c0 + 1, 4 * c0 + 2), y)
+        f(B(X[:, c0:c1, 2:4, :], "XQ", 4 * c0 + 2, 4 * c0 + 4), B(X[:, c0:c1, 0:2, :], "XQ", 4 * c0, 4 * c0 + 2))
+        f(A("XR", 64 * c0, 64 * c1), B(X[:, c0:c1, :, :], "XQ", 4 * c0, 4 * c0 + 4))
+
+    def dist(off, ps, ex, split, hooks=()):
+        for h in range(4):
+            lo, hi = 1024 * h, 1024 * h + 1024
+            end = h == 3
+            cuts = (0, 512, 1024) if split and h == 0 else (0, 1024)
+            for a, b in zip(cuts[:-1], cuts[1:]):
+                gat(A("DF", lo + a, lo + b), WIN, A(off, (lo + a) // 16, (lo + b) // 16), A("XR", a, b), OP.subtract)
+            if h < len(hooks):
+                hooks[h]()
+            out = B(T[ps][:, 0:16, 4 * h:4 * h + 4], ps, 0, 16)
+            n = 0
+            for b0 in range(4 if end else 1):
+                nm = "AD%d" % b0 if end else "ADx"
+                st = 4 if end else 1
+                act(B(T.AD[:, lo + b0:hi:st], nm, lo, hi), B(T.DF[:, lo + b0:hi:st], "DF", lo, hi), AF.Abs)
+                for b in range(b0, 16, st):
+                    mm(out, A("FS", 15 - b, 143 - b), B(T.AD[:, lo + b:hi:16], nm, lo, hi), n == 0, n == 15)
+                    n += 1
+                    if n == (4 if end else 14):
+                        for c in (0, 8):
+                            mm(B(T[ps][:, c:c + 8, 4 * h:4 * h + 4], ps, 0, 16), A("ID"), B(T[ex][:, 0:8, 4 * h:4 * h + 4], ex, 0, 8), False, False)
+
+    def latch(key, pay, res, o0, o1):
+        scan(A("FM"), A(res), key, o0, o1)
+        tt(A("RR"), key, A("FM"), OP.is_equal)
+        tt(A("D1"), pay, A("RR"), OP.subtract)
+        scan(A("LT"), A("RR"), A("D1"), OP.max, OP.min)
+
+    LAST = A("LT", 15, 256, 16)
+    FML = A("FM", 15, 256, 16)
+    DPS, EPS = A("dps"), A("eps")
+    PAE = A("kps", 128, 384)
+    PAP = A("t2", 0, 256)
+    KEY = A("mps", 256, 512)
+    for r in range(NR):
+        last = r == NR - 1
+        Y, PO, KM, PA, MK, MS = ["%s%d" % (n, r) for n in ("Y", "PO", "KM", "PA", "MK", "MS")]
+        if r:
+            for n, s in ((Y, "ry"), (PO, "rp"), (KM, "rk"), (PA, "ra")):
+                land(A(n), "%s_%d" % (s, r), prv, [core])
+        spread(Y, 0, 8, "V")
+        spread(Y, 8, 16, "S")
+        if r == 0:
+            pay0()
+        dist(PO, "dps", KM, True, (lambda: pens("KM0"), tables, lambda: pay1("PA0")) if r == 0 else ())
+        act(A("TX", 2048, 2304), A(Y), AF.Copy)
+        act(PAP, A(PA), AF.Copy)
+        cp(KEY, DPS)
+        latch(KEY, PAP, "RES", OP.mult, OP.max)
+        ts(A("PAYI"), LAST, 4194304.0, OP.mult)
+        ts(A("UVI", 0, 16), A("PAYI"), 18, SHR)
+        ts(A("UVI", 16, 32), A("PAYI"), 11, SHR, 127, AND)
+        cp(A("UVF"), A("UVI"))
+        for c in range(16):
+            lo, hi = 128 * c, 128 * c + 128
+            ts(A("OU", lo, hi), A("IU"), A("UVF", c, c + 1), OP.is_equal)
+            ts(A("OV", lo, hi), A("IV"), A("UVF", 16 + c, 17 + c), OP.is_equal)
+            mm(A("mps", 0, 128), A("OU", lo, hi), A("OV", lo, hi), c == 0, c == 15)
+        ts(A(MS), A("mps", 0, 128), 0.5, OP.is_ge)
+        send(A(MS), rest(rank), T[MK][:, 128 * rank:128 * rank + 128], "mk%d_%d" % (r, rank))
+        for j in range(NG):
+            if j != rank:
+                land(A(MK, 128 * j, 128 * j + 128), "mk%d_%d" % (r, j), T.cores[j], rest(j))
+        if r:
+            ts(A("THA"), B(T[KM][:], KM, 0, 8), 0.0, OP.is_lt, -BIG, OP.mult)
+            for h in range(2):
+                ts(A("THB", 128 * h, 128 * h + 128), A("THA"), 65536.0, OP.add)
+            tt(A("T1"), DPS, A("THB"), OP.is_ge)
+            tt(A("D1"), A("T1"), A("BIGK"), OP.mult)
+            tt(KEY, DPS, A("D1"), OP.max)
+            latch(KEY, PAP, "RES", OP.mult, OP.max)
+            ts(A("PAYI"), LAST, 4194304.0, OP.mult)
+        ts(A("TEI"), A("PAYI"), 2047, AND)
+        cp(A("TEO"), A("TEI"))
+        gat(A("A16"), A("PU"), A("TEO"))
+        t32(A("C16"), A("A16"))
+        swap("t1", "C16")
+        ts(A("PKI"), A("PAYI"), 11, SHR)
+        cp(A("PK"), A("PKI"))
+        ts(A("DKM"), FML, 16.0, OP.subtract, 65536.0, OP.min)
+        cp(A("DKI"), FML)
+        ts(A("DKJ"), A("DKI"), 15, AND)
+        offs("PDO", "t1")
+        ts(PAE, T1D, 2.0 ** -11, OP.mult, 1.0, OP.add)
+        if r == 0:
+            tables2()
+        else:
+            for h in range(4):
+                cp(B(T.PFL[:, 0:16, 4 * h:4 * h + 4], "PFL", 0, 16), A(PO, 64 * h, 64 * h + 64))
+        def bank(q, lo, hi):
+            n = "t%d" % q
+            return B(T[n][:, lo // 16:hi // 16, :], n, lo // 16, hi // 16) if q < 2 else A(n, lo, hi)
+        order = (3, 0, 2, 1)
+        for q in order:
+            mm(bank(q, 0, 512), A("ID"), A("TX", 512 * q, 512 * q + 512), True, False)
+        mm(A("kps", 0, 128), A("ID"), A(MS), True, False)
+        js = [j for j in range(NG) if j != rank]
+        for j in js:
+            mm(A("kps", 0, 128), A("ID"), A(MK, 128 * j, 128 * j + 128), False, j == js[-1])
+        ts(A("CUT"), A("kps", 0, 128), 3.5, OP.is_ge)
+        for q in order:
+            for u in range(4):
+                v = 4 * q + u
+                mm(bank(q, 128 * u, 128 * u + 128), A("REP", 128 * v, 128 * v + 128), A("CUT"), False, u == 3)
+        cp(A("BKA", 0, 256, 16), A("DKJ"))
+        scan(A("KB"), A("RES"), A("BKA"), OP.mult, OP.add)
+        for n, q in enumerate(order):
+            o = A("TX", 512 * q, 512 * q + 512)
+            if n % 2 == 0:
+                ts(o, bank(q, 0, 512), 0.0, OP.max)
+                if n == 0:
+                    tt(A("OH"), A("KB"), A("KREV"), OP.is_equal)
+            else:
+                act(o, bank(q, 0, 512), AF.Relu)
+        tt(A("T1"), A("OH"), A("PFL"), OP.mult)
+        tt(A("PZ"), A("PFL"), A("T1"), OP.subtract)
+        dist("PDO", "eps", "KFW", False)
+        if r == 0:
+            cp(A("CAC"), A("CUT"))
+        else:
+            tt(A("CA2" if r == 1 else "CAC"), A("CAC" if r == 1 else "CA2"), A("CUT"), OP.max)
+        cp(KEY, EPS)
+        latch(KEY, PAE, "RESB", OP.add, OP.min)
+        ts(A("BE"), LAST, 2048.0, OP.mult)
+        tt(A("TK"), A("DKM"), FML, OP.is_ge)
+        tt(A("O1"), A("BE"), A("BASE"), OP.subtract)
+        tt(A("N1"), A("BE"), A("PK"), OP.subtract)
+        tt(A("O2"), A("O1"), A("TK"), OP.mult)
+        tt(A("N2"), A("N1"), A("TK"), OP.mult)
+        tt(A("OF"), A("O2"), A("BASE"), OP.add)
+        tt(A("BKB", 0, 256, 16), A("N2"), A("PK"), OP.add)
+        cp(A("OFO"), A("OF"))
+        gat(A("SU"), A("TX"), A("OFO"), A(Y), OP.add)
+        e = r + 1
+        YS = "YS%d" % e
+        act(A(YS), A("SU"), scale=0.5, bias=0.25)
+        if not last:
+            send(A(YS), [nxt], T["Y%d" % e][:], "ry_%d" % e)
+        NB, NV = A("mps", 0, 256), A("mps", 256, 512)
+        scan(NB, A("RES"), A("BKB"), OP.mult, OP.add)
+        tt(NV, A("OH"), NB, OP.mult)
+        if not last:
+            tt(A("PFL"), A("PZ"), NV, OP.add)
+            offs("POS%d" % e, "PFL")
+            send(A("POS%d" % e), [nxt], T["PO%d" % e][:], "rp_%d" % e)
+            pay0()
+            pens("KMS%d" % e)
+            pay1("PAS%d" % e)
+            send(A("KMS%d" % e), [nxt], T["KM%d" % e][:], "rk_%d" % e)
+            send(A("PAS%d" % e), [nxt], T["PA%d" % e][:], "ra_%d" % e)
+        else:
+            tt(A("PNH"), A("PZ"), NV, OP.add)
+            swap("t1", "PNH")
+            for h in range(2):
+                act(A("YXB", h, 256, 2), A(YS, 128 * h, 128 * h + 128), scale=-1.0, bias=256.0)
+            store("Y", T.yx[:], A("YXB"), "oyx")
+            store("Y", T.yc[:], A("CAC"), "oyc")
+            t32(A("YPA"), T1D)
+            cp(A("YPB", 0, 256, 2), A("YPA", 0, 128))
+            act(A("YPB", 1, 256, 2), A("YPA", 128, 256), AF.Copy)
+            store("Y", T.yp[:], A("YPB"), "oyp")
+
+    for s in ["oyp", "oyx", "oyc"] + LOADS:
+        g.sync.wait_ge(T.sem[s], 16)
+    g.wait_ge(T.sem.loc, sent[0])
+    for q in ("V", "S", "P", "G"):
+        g.wait_ge(T.sem[SEM[q]], cnt[q])

@@ -10,31 +10,30 @@ F4, BF, HF, I4, U2 = "float32", "bfloat16", "float16", "int32", "uint16"
 SCRATCH = {}
 for _n, _w, _d in (
         ("TXR", 2048, BF), ("TX", 2304, BF), ("PU", 2048, I4), ("P0R", 256, I4), ("X0R", 256, BF),
-        ("XR", 1024, BF), ("DF", 4096, BF), ("AD", 4096, BF), ("OU", 2048, BF), ("OV", 2048, BF),
-        ("PI", 8, I4), ("PF", 12, F4), ("IF", 144, F4), ("MU", 128, F4), ("MG", 128, F4), ("FS", 144, BF), ("ID", 128, BF), ("SW", 512, HF),
-        ("ONB", 128, BF), ("ONF", 256, F4), ("NEGC", 128, F4), ("BGC", 256, F4), ("REP", 2048, BF), ("BD", 128, BF), ("H16", 16, F4),
-        ("IU", 128, BF), ("IV", 128, BF), ("BDM", 128, F4), ("KREV", 256, F4), ("KRV0", 128, F4), ("NEGM", 128, F4), ("RES", 256, F4),
-        ("RES1", 256, F4), ("RESB", 256, F4), ("BIGK", 256, F4), ("BASE", 16, F4), ("BKA", 256, F4), ("BKB", 256, F4),
-        ("A16", 256, HF), ("FM", 256, F4), ("RR", 256, F4), ("D1", 256, F4), ("LT", 256, F4), ("PAYI", 16, I4), ("UVI", 32, I4), ("UVF", 32, F4),
-        ("TEI", 16, I4), ("TEO", 16, U2), ("PKI", 16, I4), ("PK", 16, F4), ("DKM", 16, F4), ("DKI", 16, I4), ("DKJ", 16, I4), ("KB", 256, F4),
-        ("OH", 256, F4), ("PZ", 256, F4), ("THA", 128, F4), ("THB", 256, F4), ("T1", 256, F4), ("PDO", 256, U2), ("CUT", 128, BF),
-        ("CAC", 128, F4), ("CA2", 128, F4), ("BE", 16, F4), ("TK", 16, F4), ("O1", 16, F4), ("O2", 16, F4), ("OF", 16, F4), ("OFO", 16, U2),
+        ("XR", 1024, BF), ("DF", 4096, BF), ("AD", 4096, BF), ("TG", 512, BF), ("OU", 2048, BF), ("OV", 2048, BF),
+        ("PI", 8, I4), ("PF", 12, F4), ("IF", 144, F4), ("MU", 128, F4), ("MG", 128, F4), ("FS", 144, BF), ("ID", 128, BF), ("NID", 128, BF),
+        ("SW", 512, HF), ("ONB", 128, BF), ("ONF", 256, F4), ("NEGC", 128, F4), ("BGC", 256, F4), ("REP", 2048, BF), ("BD", 128, BF),
+        ("H16", 16, F4), ("IU", 128, BF), ("IV", 128, BF), ("BDM", 128, F4), ("KREV", 256, F4), ("KFW", 128, BF), ("KRV0", 128, F4),
+        ("NEGM", 128, F4), ("RES", 256, F4), ("RES1", 256, F4), ("RESB", 256, F4), ("BIGK", 256, F4), ("BASE", 16, F4), ("BKA", 256, F4), ("BKB", 256, F4),
+        ("A16", 256, HF), ("PFL", 256, F4), ("FM", 256, F4), ("RR", 256, F4), ("D1", 256, F4), ("LT", 256, F4), ("PAYI", 16, I4), ("UVI", 32, I4),
+        ("UVF", 32, F4), ("TEI", 16, I4), ("TEO", 16, U2), ("PKI", 16, I4), ("PK", 16, F4), ("DKM", 16, F4), ("DKI", 16, I4), ("DKJ", 16, I4),
+        ("PZ", 256, F4), ("THA", 128, F4), ("THB", 256, F4), ("T1", 256, F4), ("PDO", 256, U2), ("CUT", 128, BF),
+        ("CAC", 128, F4), ("CA2", 128, F4), ("TK", 16, F4), ("O1", 16, F4), ("O2", 16, F4), ("OF", 16, F4), ("OFO", 16, U2),
         ("N1", 16, F4), ("N2", 16, F4), ("SU", 256, F4), ("EQ", 128, F4), ("PRE", 128, F4), ("PM", 128, F4), ("TA", 256, F4), ("TB", 256, F4),
         ("YPA", 256, F4), ("YPB", 256, F4), ("YXB", 256, BF)):
     SCRATCH[_n] = ("sbuf", [128, _w], _d)
 SCRATCH["XQ"] = ("sbuf", [128, 16, 4, 16], BF)
-for _n, _c, _d in (("C16", 16, HF), ("PNH", 16, HF), ("PFL", 16, F4), ("KFW", 8, BF)):
-    SCRATCH[_n] = ("sbuf", [128, _c, 16], _d)
-for _n, _c in (("dps", 16), ("eps", 16), ("t0", 32), ("t1", 32)):
-    SCRATCH[_n] = ("psum", [128, _c, 16], F4)
-for _n in ("mps", "kps", "t2", "t3"):
+for _n in ("C16", "PNH"):
+    SCRATCH[_n] = ("sbuf", [128, 16, 16], HF)
+SCRATCH["sps"] = ("psum", [128, 32, 16], F4)
+for _n in ("dps", "eps", "kps", "t0", "t1", "t2", "t3"):
     SCRATCH[_n] = ("psum", [128, 512], F4)
 for _r in range(NR):
     SCRATCH["Y%d" % _r] = ("sbuf", [128, 256], BF)
     SCRATCH["YS%d" % (_r + 1)] = ("sbuf", [128, 256], BF)
     for _s in ("", "S") if _r else ("",):
         SCRATCH["PO%s%d" % (_s, _r)] = ("sbuf", [128, 256], U2)
-        SCRATCH["KM%s%d" % (_s, _r)] = ("sbuf", [128, 8, 16], BF)
+        SCRATCH["KM%s%d" % (_s, _r)] = ("sbuf", [128, 128], BF)
         SCRATCH["PA%s%d" % (_s, _r)] = ("sbuf", [128, 256], F4)
     SCRATCH["MK%d" % _r] = ("sbuf", [128, 1024], BF)
     SCRATCH["MS%d" % _r] = ("sbuf", [128, 128], BF)
@@ -188,6 +187,7 @@ def rank_program(g, core, T, topo):
     iota(A("IF"), [[1, 144]], 0, 0)
     iota(A("ONB"), [[0, 128]], 1, 0)
     keep(A("ID"), A("ONB"), [[-1, 128]], OP.is_equal, 0.0, 0, 1)
+    act(A("NID"), A("ID"), scale=-1.0)
     iota(A("KREV"), [[0, 16], [-1, 16]], 15, 0)
     keep(A("KRV0"), A("KREV", 0, 128), [[0, 8], [1, 16]], OP.is_gt, -BIG, 0, 0)
     iota(A("ONF"), [[0, 256]], 1, 0)
@@ -206,7 +206,6 @@ def rank_program(g, core, T, topo):
     iota(A("BKB"), [[0, 256]], 0, 0)
     iota(A("BGC"), [[0, 16], [-1, 16]], 262144 + 15, 0)
     keep(A("BIGK"), A("BGC"), CK, OP.is_gt, 0.0, 0, 0)
-    act(A("RESB"), A("RES1"), scale=1048576.0)
     AND, SHR = OP.bitwise_and, OP.arith_shift_right
     ts(A("PI", 1, 2), A("PI", 0, 1), 15, AND)
     ts(A("PI", 2, 3), A("PI", 0, 1), 4, SHR)
@@ -229,31 +228,40 @@ def rank_program(g, core, T, topo):
                 j = 2 * x + y
                 mm(B(T[dst][:, x:16:2, :], dst, 0, 16), A("SW", 128 * j, 128 * j + 128), B(T[src][:, y:16:2, :], src, 0, 16), y == 0, y == 1)
 
-    def offs(o, sn):
+    def offs(o):
         for h in range(4):
-            cp(A(o, 64 * h, 64 * h + 64), B(T[sn][:, 0:16, 4 * h:4 * h + 4], sn, 0, 16))
+            ts(A(o, 64 * h, 64 * h + 64), A("PFL", h, 256, 4), 2048.0, OP.mult)
 
+    def spread(yn, c0, c1, q):
+        f = cp if q == "V" else (lambda o, i: act(o, i, AF.Copy))
+        X, y = T.XQ, A(yn, 16 * c0, 16 * c1)
+        f(B(X[:, c0:c1, 0, :], "XQ", 4 * c0, 4 * c0 + 1), y)
+        f(B(X[:, c0:c1, 1, :], "XQ", 4 * c0 + 1, 4 * c0 + 2), y)
+        f(B(X[:, c0:c1, 2:4, :], "XQ", 4 * c0 + 2, 4 * c0 + 4), B(X[:, c0:c1, 0:2, :], "XQ", 4 * c0, 4 * c0 + 2))
+        f(A("XR", 64 * c0, 64 * c1), B(X[:, c0:c1, :, :], "XQ", 4 * c0, 4 * c0 + 4))
+
+    for h in range(2):
+        ts(A("Y0", 128 * h, 128 * h + 128), A("X0R", h, 256, 2), -1.0, OP.mult, 256.0, OP.add)
+    spread("Y0", 0, 8, "V")
+    spread("Y0", 8, 16, "S")
     for h in range(2):
         cp(A("A16", 128 * h, 128 * h + 128), A("P0R", h, 256, 2))
     t32(A("C16"), A("A16"))
-    swap("t1", "C16")
-    T1D = B(T.t1[:, 0:16, :], "t1", 0, 16)
-    offs("PO0", "t1")
-    cp(A("PFL"), T1D)
-    for h in range(2):
-        ts(A("Y0", 128 * h, 128 * h + 128), A("X0R", h, 256, 2), -1.0, OP.mult, 256.0, OP.add)
+    swap("sps", "C16")
+    SD = B(T.sps[:, 0:16, :], "sps", 0, 16)
+    ts(A("PFL"), SD, 2.0 ** -11, OP.mult)
+    offs("PO0")
     ts(A("FS"), A("IF"), col(10), OP.is_equal, 32.0, OP.mult)
 
     def pay0():
-        act(A("TA"), A("PFL"), scale=2.0 ** -11, bias=1.0)
-        act(A("TB"), A("PFL"), scale=2.0 ** -22)
+        act(A("TA"), A("PFL"), bias=1.0)
+        act(A("TB"), A("PFL"), scale=2.0 ** -11)
 
     def pay1(pa):
         tt(A(pa, 1, 256), A("TA", 1, 256), A("TB", 0, 255), OP.add)
 
     def pens(km):
-        P = T.PFL
-        tt(A("EQ"), B(P[:, 0:8, :], "PFL", 0, 8), B(P[:, 8:16, :], "PFL", 8, 16), OP.is_equal)
+        tt(A("EQ"), A("PFL", 0, 128), A("PFL", 128, 256), OP.is_equal)
         scan(A("PRE"), A("RES1", 0, 128), A("EQ"), OP.max, OP.min)
         tt(A("PM"), A("PRE"), A("NEGM"), OP.mult)
         tt(A(km), A("PM"), A("KRV0"), OP.add)
@@ -278,37 +286,33 @@ def rank_program(g, core, T, topo):
         for u in range(16):
             ts(A("REP", 128 * u, 128 * u + 128), A("BD"), A("H16", u, u + 1), OP.mult)
         ts(A("O1"), A("BASE"), col(1), OP.add)
-        cp(A("BASE"), A("O1"))
+        ts(A("BASE"), A("O1"), 2.0 ** -11, OP.mult)
 
-    def spread(yn, c0, c1, q):
-        f = cp if q == "V" else (lambda o, i: act(o, i, AF.Copy))
-        X, y = T.XQ, A(yn, 16 * c0, 16 * c1)
-        f(B(X[:, c0:c1, 0, :], "XQ", 4 * c0, 4 * c0 + 1), y)
-        f(B(X[:, c0:c1, 1, :], "XQ", 4 * c0 + 1, 4 * c0 + 2), y)
-        f(B(X[:, c0:c1, 2:4, :], "XQ", 4 * c0 + 2, 4 * c0 + 4), B(X[:, c0:c1, 0:2, :], "XQ", 4 * c0, 4 * c0 + 2))
-        f(A("XR", 64 * c0, 64 * c1), B(X[:, c0:c1, :, :], "XQ", 4 * c0, 4 * c0 + 4))
-
-    def dist(off, ps, ex, split, hooks=()):
+    def dist(off, ps, ex, hooks=()):
+        do("S", lambda: g.scalar.activation(T.TG[:], T.TX[:, 0:2048].indirect(T[off][:, 32:64]), AF.Copy, bias=0.0, scale=1.0),
+           [A("TG")], [WIN, A(off, 32, 64)])
+        mm(A("t3"), A("ID"), A("TG"), True, False)
+        mm(A("t3"), A("NID"), A("XR", 512, 1024), False, True)
         for h in range(4):
             lo, hi = 1024 * h, 1024 * h + 1024
-            end = h == 3
-            cuts = (0, 512, 1024) if split and h == 0 else (0, 1024)
-            for a, b in zip(cuts[:-1], cuts[1:]):
-                gat(A("DF", lo + a, lo + b), WIN, A(off, (lo + a) // 16, (lo + b) // 16), A("XR", a, b), OP.subtract)
+            m = hi if h else lo + 512
+            gat(A("DF", lo, m), WIN, A(off, lo // 16, m // 16), A("XR", 0, m - lo), OP.subtract)
             if h < len(hooks):
                 hooks[h]()
-            out = B(T[ps][:, 0:16, 4 * h:4 * h + 4], ps, 0, 16)
+            out = A(ps, h, 256, 4)
+            st = (1, 2, 2, 4)[h]
             n = 0
-            for b0 in range(4 if end else 1):
-                nm = "AD%d" % b0 if end else "ADx"
-                st = 4 if end else 1
-                act(B(T.AD[:, lo + b0:hi:st], nm, lo, hi), B(T.DF[:, lo + b0:hi:st], "DF", lo, hi), AF.Abs)
+            for b0 in range(st):
+                nm = "AD%d_%d" % (h, b0)
+                act(B(T.AD[:, lo + b0:m:st], nm, lo, m), B(T.DF[:, lo + b0:m:st], "DF", lo, m), AF.Abs)
+                if h == 0:
+                    act(B(T.AD[:, m:hi], nm, m, hi), A("t3"), AF.Abs)
                 for b in range(b0, 16, st):
                     mm(out, A("FS", 15 - b, 143 - b), B(T.AD[:, lo + b:hi:16], nm, lo, hi), n == 0, n == 15)
                     n += 1
-                    if n == (4 if end else 14):
-                        for c in (0, 8):
-                            mm(B(T[ps][:, c:c + 8, 4 * h:4 * h + 4], ps, 0, 16), A("ID"), B(T[ex][:, 0:8, 4 * h:4 * h + 4], ex, 0, 8), False, False)
+                    if n == (4 if h == 3 else 14):
+                        for c in (0, 128):
+                            mm(A(ps, c + h, c + 128, 4), A("ID"), A(ex, h, 128, 4), False, False)
 
     def latch(key, pay, res, o0, o1):
         scan(A("FM"), A(res), key, o0, o1)
@@ -318,25 +322,35 @@ def rank_program(g, core, T, topo):
 
     LAST = A("LT", 15, 256, 16)
     FML = A("FM", 15, 256, 16)
-    DPS, EPS = A("dps"), A("eps")
+    DPS, EPS = A("dps", 0, 256), A("eps", 0, 256)
     PAE = A("kps", 128, 384)
     PAP = A("t2", 0, 256)
-    KEY = A("mps", 256, 512)
+    BGP = A("eps", 256, 512)
+    MPS = A("dps", 256, 384)
+    OH = A("dps", 256, 512)
+    PX = A("t0", 0, 256)
     for r in range(NR):
         last = r == NR - 1
         Y, PO, KM, PA, MK, MS = ["%s%d" % (n, r) for n in ("Y", "PO", "KM", "PA", "MK", "MS")]
         if r:
             for n, s in ((Y, "ry"), (PO, "rp"), (KM, "rk"), (PA, "ra")):
                 land(A(n), "%s_%d" % (s, r), prv, [core])
-        spread(Y, 0, 8, "V")
-        spread(Y, 8, 16, "S")
-        if r == 0:
+        if r:
+            spread(Y, 0, 8, "V")
+            spread(Y, 8, 16, "S")
+        else:
             pay0()
-        dist(PO, "dps", KM, True, (lambda: pens("KM0"), tables, lambda: pay1("PA0")) if r == 0 else ())
+        dist(PO, "dps", KM, (lambda: pens("KM0"), tables, lambda: pay1("PA0")) if r == 0 else ())
         act(A("TX", 2048, 2304), A(Y), AF.Copy)
         act(PAP, A(PA), AF.Copy)
-        cp(KEY, DPS)
-        latch(KEY, PAP, "RES", OP.mult, OP.max)
+        if r == 0:
+            act(A("RESB"), A("RES1"), scale=1048576.0)
+            act(BGP, A("BIGK"), AF.Copy)
+        else:
+            act(A("THA"), A(KM), AF.Relu, scale=-1.0)
+            for h in range(2):
+                act(A("THB", 128 * h, 128 * h + 128), A("THA"), scale=-1.0, bias=65536.0)
+        latch(DPS, PAP, "RES", OP.mult, OP.max)
         ts(A("PAYI"), LAST, 4194304.0, OP.mult)
         ts(A("UVI", 0, 16), A("PAYI"), 18, SHR)
         ts(A("UVI", 16, 32), A("PAYI"), 11, SHR, 127, AND)
@@ -345,41 +359,37 @@ def rank_program(g, core, T, topo):
             lo, hi = 128 * c, 128 * c + 128
             ts(A("OU", lo, hi), A("IU"), A("UVF", c, c + 1), OP.is_equal)
             ts(A("OV", lo, hi), A("IV"), A("UVF", 16 + c, 17 + c), OP.is_equal)
-            mm(A("mps", 0, 128), A("OU", lo, hi), A("OV", lo, hi), c == 0, c == 15)
-        ts(A(MS), A("mps", 0, 128), 0.5, OP.is_ge)
+            mm(MPS, A("OU", lo, hi), A("OV", lo, hi), c == 0, c == 15)
+        ts(A(MS), MPS, 0.5, OP.is_ge)
         send(A(MS), rest(rank), T[MK][:, 128 * rank:128 * rank + 128], "mk%d_%d" % (r, rank))
         for j in range(NG):
             if j != rank:
                 land(A(MK, 128 * j, 128 * j + 128), "mk%d_%d" % (r, j), T.cores[j], rest(j))
         if r:
-            ts(A("THA"), B(T[KM][:], KM, 0, 8), 0.0, OP.is_lt, -BIG, OP.mult)
-            for h in range(2):
-                ts(A("THB", 128 * h, 128 * h + 128), A("THA"), 65536.0, OP.add)
             tt(A("T1"), DPS, A("THB"), OP.is_ge)
-            tt(A("D1"), A("T1"), A("BIGK"), OP.mult)
-            tt(KEY, DPS, A("D1"), OP.max)
-            latch(KEY, PAP, "RES", OP.mult, OP.max)
+            tt(A("D1"), A("T1"), BGP, OP.mult)
+            tt(DPS, DPS, A("D1"), OP.max)
+            latch(DPS, PAP, "RES", OP.mult, OP.max)
             ts(A("PAYI"), LAST, 4194304.0, OP.mult)
         ts(A("TEI"), A("PAYI"), 2047, AND)
         cp(A("TEO"), A("TEI"))
         gat(A("A16"), A("PU"), A("TEO"))
         t32(A("C16"), A("A16"))
-        swap("t1", "C16")
-        ts(A("PKI"), A("PAYI"), 11, SHR)
-        cp(A("PK"), A("PKI"))
-        ts(A("DKM"), FML, 16.0, OP.subtract, 65536.0, OP.min)
+        swap("sps", "C16")
         cp(A("DKI"), FML)
+        ts(A("PKI"), A("PAYI"), 11, SHR)
         ts(A("DKJ"), A("DKI"), 15, AND)
-        offs("PDO", "t1")
-        ts(PAE, T1D, 2.0 ** -11, OP.mult, 1.0, OP.add)
+        ts(A("PK"), A("PKI"), 2.0 ** -11, OP.mult)
+        ts(A("DKM"), FML, 16.0, OP.subtract, 65536.0, OP.min)
+        cp(A("BKA", 0, 256, 16), A("DKJ"))
         if r == 0:
             tables2()
         else:
             for h in range(4):
-                cp(B(T.PFL[:, 0:16, 4 * h:4 * h + 4], "PFL", 0, 16), A(PO, 64 * h, 64 * h + 64))
+                ts(A("PFL", h, 256, 4), A(PO, 64 * h, 64 * h + 64), 2.0 ** -11, OP.mult)
+        scan(OH, A("RES"), A("BKA"), OP.mult, OP.add)
         def bank(q, lo, hi):
-            n = "t%d" % q
-            return B(T[n][:, lo // 16:hi // 16, :], n, lo // 16, hi // 16) if q < 2 else A(n, lo, hi)
+            return A("t%d" % q, lo, hi)
         order = (3, 0, 2, 1)
         for q in order:
             mm(bank(q, 0, 512), A("ID"), A("TX", 512 * q, 512 * q + 512), True, False)
@@ -392,46 +402,45 @@ def rank_program(g, core, T, topo):
             for u in range(4):
                 v = 4 * q + u
                 mm(bank(q, 128 * u, 128 * u + 128), A("REP", 128 * v, 128 * v + 128), A("CUT"), False, u == 3)
-        cp(A("BKA", 0, 256, 16), A("DKJ"))
-        scan(A("KB"), A("RES"), A("BKA"), OP.mult, OP.add)
+        for h in range(4):
+            cp(A("PDO", 64 * h, 64 * h + 64), B(T.sps[:, 0:16, h:16:4], "sps", 0, 16))
         for n, q in enumerate(order):
             o = A("TX", 512 * q, 512 * q + 512)
             if n % 2 == 0:
                 ts(o, bank(q, 0, 512), 0.0, OP.max)
                 if n == 0:
-                    tt(A("OH"), A("KB"), A("KREV"), OP.is_equal)
+                    tt(OH, OH, A("KREV"), OP.is_equal)
             else:
                 act(o, bank(q, 0, 512), AF.Relu)
-        tt(A("T1"), A("OH"), A("PFL"), OP.mult)
-        tt(A("PZ"), A("PFL"), A("T1"), OP.subtract)
-        dist("PDO", "eps", "KFW", False)
+        dist("PDO", "eps", "KFW")
         if r == 0:
             cp(A("CAC"), A("CUT"))
         else:
             tt(A("CA2" if r == 1 else "CAC"), A("CAC" if r == 1 else "CA2"), A("CUT"), OP.max)
-        cp(KEY, EPS)
-        latch(KEY, PAE, "RESB", OP.add, OP.min)
-        ts(A("BE"), LAST, 2048.0, OP.mult)
+        ts(PAE, SD, 2.0 ** -11, OP.mult, 1.0, OP.add)
+        tt(PX, OH, A("PFL"), OP.mult)
+        tt(A("PZ"), A("PFL"), PX, OP.subtract)
+        latch(EPS, PAE, "RESB", OP.add, OP.min)
+        tt(A("O1"), LAST, A("BASE"), OP.subtract)
         tt(A("TK"), A("DKM"), FML, OP.is_ge)
-        tt(A("O1"), A("BE"), A("BASE"), OP.subtract)
-        tt(A("N1"), A("BE"), A("PK"), OP.subtract)
+        tt(A("N1"), LAST, A("PK"), OP.subtract)
         tt(A("O2"), A("O1"), A("TK"), OP.mult)
         tt(A("N2"), A("N1"), A("TK"), OP.mult)
         tt(A("OF"), A("O2"), A("BASE"), OP.add)
         tt(A("BKB", 0, 256, 16), A("N2"), A("PK"), OP.add)
-        cp(A("OFO"), A("OF"))
+        ts(A("OFO"), A("OF"), 2048.0, OP.mult)
         gat(A("SU"), A("TX"), A("OFO"), A(Y), OP.add)
         e = r + 1
         YS = "YS%d" % e
         act(A(YS), A("SU"), scale=0.5, bias=0.25)
         if not last:
             send(A(YS), [nxt], T["Y%d" % e][:], "ry_%d" % e)
-        NB, NV = A("mps", 0, 256), A("mps", 256, 512)
+        NB, NV = A("T1"), A("t0", 256, 512)
         scan(NB, A("RES"), A("BKB"), OP.mult, OP.add)
-        tt(NV, A("OH"), NB, OP.mult)
+        tt(NV, OH, NB, OP.mult)
         if not last:
             tt(A("PFL"), A("PZ"), NV, OP.add)
-            offs("POS%d" % e, "PFL")
+            offs("POS%d" % e)
             send(A("POS%d" % e), [nxt], T["PO%d" % e][:], "rp_%d" % e)
             pay0()
             pens("KMS%d" % e)
@@ -440,14 +449,14 @@ def rank_program(g, core, T, topo):
             send(A("PAS%d" % e), [nxt], T["PA%d" % e][:], "ra_%d" % e)
         else:
             tt(A("PNH"), A("PZ"), NV, OP.add)
-            swap("t1", "PNH")
+            swap("sps", "PNH")
             for h in range(2):
                 act(A("YXB", h, 256, 2), A(YS, 128 * h, 128 * h + 128), scale=-1.0, bias=256.0)
             store("Y", T.yx[:], A("YXB"), "oyx")
             store("Y", T.yc[:], A("CAC"), "oyc")
-            t32(A("YPA"), T1D)
-            cp(A("YPB", 0, 256, 2), A("YPA", 0, 128))
-            act(A("YPB", 1, 256, 2), A("YPA", 128, 256), AF.Copy)
+            t32(A("YPA"), SD)
+            ts(A("YPB", 0, 256, 2), A("YPA", 0, 128), 2048.0, OP.mult)
+            act(A("YPB", 1, 256, 2), A("YPA", 128, 256), scale=2048.0)
             store("Y", T.yp[:], A("YPB"), "oyp")
 
     for s in ["oyp", "oyx", "oyc"] + LOADS:

from concourse.bass import DstId, RemoteDMATransfer
from concourse.mybir import dt, AluOpType as OP, ActivationFunctionType as AF

NR = 3
STEP = 5
NG = 8
BIG = 262144.0

F4, BF, HF, I4, U2 = "float32", "bfloat16", "float16", "int32", "uint16"
SCRATCH = {}
for _n, _w, _d in (
        ("TXR", 2048, BF), ("TX", 2304, BF), ("PU", 2048, I4), ("P0R", 256, I4), ("X0R", 256, BF),
        ("XR", 1024, BF), ("DF", 4096, BF), ("AD", 4096, BF), ("TG", 512, BF), ("OU", 2048, BF), ("OV", 2048, BF),
        ("PI", 8, I4), ("PF", 12, F4), ("IF", 144, F4), ("MU", 128, F4), ("MG", 128, F4), ("FS", 144, BF), ("ID", 128, BF), ("NID", 128, BF),
        ("SW", 512, HF), ("ONB", 128, BF), ("ONF", 256, F4), ("NEGC", 128, F4), ("BGC", 256, F4), ("REP", 2048, BF), ("BD", 128, BF),
        ("H16", 16, F4), ("IU", 128, BF), ("IV", 128, BF), ("BDM", 128, F4), ("KREV", 256, F4), ("KFW", 128, BF), ("KRV0", 128, F4),
        ("NEGM", 128, F4), ("RES", 256, F4), ("RES1", 256, F4), ("RESB", 256, F4), ("BIGK", 256, F4), ("BASE", 16, F4), ("BKA", 256, F4), ("BKB", 256, F4),
        ("A16", 256, HF), ("PFL", 256, F4), ("FM", 256, F4), ("RR", 256, F4), ("D1", 256, F4), ("LT", 256, F4), ("PAYI", 16, I4), ("UVI", 32, I4),
        ("UVF", 32, F4), ("TEI", 16, I4), ("TEO", 16, U2), ("PKI", 16, I4), ("PK", 16, F4), ("DKM", 16, F4), ("DKI", 16, I4), ("DKJ", 16, I4),
        ("PZ", 256, F4), ("THA", 128, F4), ("THB", 256, F4), ("T1", 256, F4), ("PDO", 256, U2), ("CUT", 128, BF),
        ("CAC", 128, F4), ("CA2", 128, F4), ("TK", 16, F4), ("O1", 16, F4), ("O2", 16, F4), ("OF", 16, F4), ("OFO", 16, U2),
        ("N1", 16, F4), ("N2", 16, F4), ("SU", 256, F4), ("EQ", 128, F4), ("PRE", 128, F4), ("PM", 128, F4), ("TA", 256, F4), ("TB", 256, F4),
        ("YPA", 256, F4), ("YPB", 256, F4), ("YXB", 256, BF)):
    SCRATCH[_n] = ("sbuf", [128, _w], _d)
SCRATCH["XQ"] = ("sbuf", [128, 16, 4, 16], BF)
for _n in ("C16", "PNH"):
    SCRATCH[_n] = ("sbuf", [128, 16, 16], HF)
SCRATCH["sps"] = ("psum", [128, 32, 16], F4)
for _n in ("dps", "eps", "kps", "t0", "t1", "t2", "t3"):
    SCRATCH[_n] = ("psum", [128, 512], F4)
for _r in range(NR):
    SCRATCH["Y%d" % _r] = ("sbuf", [128, 256], BF)
    SCRATCH["YS%d" % (_r + 1)] = ("sbuf", [128, 256], BF)
    for _s in ("", "S") if _r else ("",):
        SCRATCH["PO%s%d" % (_s, _r)] = ("sbuf", [128, 256], U2)
        SCRATCH["KM%s%d" % (_s, _r)] = ("sbuf", [128, 128], BF)
        SCRATCH["PA%s%d" % (_s, _r)] = ("sbuf", [128, 256], F4)
    SCRATCH["MK%d" % _r] = ("sbuf", [128, 1024], BF)
    SCRATCH["MS%d" % _r] = ("sbuf", [128, 128], BF)
PSUM = [n for n in SCRATCH if SCRATCH[n][0] == "psum"]

LOADS = ["lp0", "lx0", "ltx0", "ltx1", "ltx2", "ltx3", "lpu0", "lpu1"]
SEMAPHORES = (["qv", "qs", "qp", "qg", "loc", "oyp", "oyx", "oyc"] + LOADS + ["mk%d_%d" % (r, j) for r in range(NR) for j in range(NG)]
              + ["%s_%d" % (n, r) for r in range(1, NR) for n in ("ry", "rp", "rk", "ra")])


def rank_program(g, core, T, topo):
    rank = T.rank_of(core)
    if rank is None:
        return
    Q = {"V": g.vector, "S": g.scalar, "P": g.tensor, "G": g, "Y": g.sync}
    SEM = {"V": "qv", "S": "qs", "P": "qp", "G": "qg"}
    cnt = {"V": 0, "S": 0, "P": 0, "G": 0}
    known = {q: {} for q in Q}
    acc = {}
    sent = [0]

    def A(n, lo=0, hi=None, st=1):
        hi = SCRATCH[n][1][1] if hi is None else hi
        return (T[n][:, lo:hi] if st == 1 else T[n][:, lo:hi:st], n, lo, hi)

    def B(ap, n, lo, hi):
        return (ap, n, lo, hi)

    def need(q, ins, outs):
        w = {}
        for isw, ops in ((False, ins), (True, outs)):
            for (_, n, lo, hi) in ops:
                for (l2, h2, w2, q2, s2, v2) in acc.get(n, ()):
                    ps = n in PSUM
                    if ps and q2 == q and q == "P":
                        continue
                    hit = ps and q2 != q
                    hit = hit or ((isw or w2) and lo < h2 and l2 < hi)
                    if hit and known[q].get(s2, 0) < v2:
                        w[s2] = max(w.get(s2, 0), v2)
        for s in sorted(w):
            Q[q].wait_ge(T.sem[s], w[s])
            known[q][s] = w[s]

    def note(q, s, v, ins, outs):
        for (_, n, lo, hi) in outs:
            acc[n] = [e for e in acc.get(n, []) if (e[3] == q or n not in PSUM) and not (lo <= e[0] and e[1] <= hi)]
            acc[n].append((lo, hi, True, q, s, v))
        for (_, n, lo, hi) in ins:
            acc.setdefault(n, []).append((lo, hi, False, q, s, v))

    def do(q, f, outs, ins):
        need(q, ins, outs)
        f().then_inc(T.sem[SEM[q]], 1)
        cnt[q] += 1
        note(q, SEM[q], cnt[q], ins, outs)

    def cp(o, i):
        do("V", lambda: g.vector.tensor_copy(o[0], i[0]), [o], [i])

    def tt(o, a, b, op):
        do("V", lambda: g.vector.tensor_tensor(o[0], a[0], b[0], op), [o], [a, b])

    def ts(o, a, s1, op0, s2=None, op1=None):
        extra = [s for s in (s1, s2) if isinstance(s, tuple)]
        v1 = s1[0] if isinstance(s1, tuple) else s1
        v2 = s2[0] if isinstance(s2, tuple) else s2
        if op1 is None:
            do("V", lambda: g.vector.tensor_scalar(o[0], a[0], v1, None, op0), [o], [a] + extra)
        else:
            do("V", lambda: g.vector.tensor_scalar(o[0], a[0], v1, v2, op0, op1), [o], [a] + extra)

    def scan(o, d0, d1, op0, op1):
        do("V", lambda: g.vector.tensor_tensor_scan(o[0], d0[0], d1[0], 0.0, op0, op1), [o], [d0, d1])

    def t32(o, i):
        do("V", lambda: g.vector.transpose(o[0], i[0]), [o], [i])

    def gat(o, win, off, in1=None, op=None):
        ap = win[0].indirect(off[0])
        if in1 is None:
            do("V", lambda: g.vector.tensor_copy(o[0], ap), [o], [win, off])
        else:
            do("V", lambda: g.vector.tensor_tensor(o[0], ap, in1[0], op), [o], [win, off, in1])

    def act(o, i, func=AF.Identity, scale=1.0, bias=0.0):
        do("S", lambda: g.scalar.activation(o[0], i[0], func, bias=bias, scale=scale), [o], [i])

    def mm(o, l, r, start, stop):
        do("P", lambda: g.tensor.matmul(o[0], l[0], r[0], start, stop), [o], [l, r])

    def iota(o, pat, base, cm):
        if SCRATCH[o[1]][2] == I4:
            do("G", lambda: g.iota(o[0], pat, base, cm), [o], [])
        else:
            do("G", lambda: g.iota(o[0], pat, base, cm, allow_small_or_imprecise_dtypes=True), [o], [])

    def keep(o, i, pat, cmp, fill, base, cm):
        do("G", lambda: g.affine_select(o[0], i[0], pat, cmp, fill, base, cm), [o], [i])

    def load(q, o, src, sem):
        Q[q].dma_start(o[0], src).then_inc(T.sem[sem], 16)
        note(q, sem, 16, [], [o])

    def store(q, dst, i, sem):
        need(q, [i], [])
        Q[q].dma_start(dst, i[0]).then_inc(T.sem[sem], 16)

    def engs(src, dsts):
        e = [x for x in topo.engines(src, dsts[0]) if all(x in topo.engines(src, d) for d in dsts)]
        n = 1
        while 2 * n <= min(len(e), 8):
            n *= 2
        return e[:n]

    def send(i, dsts, out, sem):
        need("G", [i], [])
        e = engs(core, dsts)
        m = 0
        for x in e:
            m |= 1 << x
        ids = []
        for d in dsts:
            rid, pid = topo.addr(d, core)
            ids.append(DstId(rid=rid, pnc=pid))
        g.remote_dma_fused([RemoteDMATransfer(dst_ids=ids, dma_engine_mask=m, remote_sem=T.sem[sem], srcs=[i[0]], dsts=[out for d in dsts])],
                           local_sem=T.sem.loc)
        sent[0] += len(e)

    def land(o, sem, src, dsts):
        note("R", sem, len(engs(src, dsts)), [], [o])

    nxt = T.cores[(rank + STEP) % NG]
    prv = T.cores[(rank - STEP) % NG]

    def rest(j):
        return [c for c in T.cores if c != T.cores[j]]

    load("Y", A("P0R"), T.p0[:], "lp0")
    load("S", A("X0R"), T.x0[:], "lx0")
    for j in range(4):
        load("Y" if j % 2 == 0 else "S", A("TXR", 512 * j, 512 * j + 512), T.tx[:, 512 * j:512 * j + 512], "ltx%d" % j)
    for j in range(2):
        load("Y", A("PU", 1024 * j, 1024 * j + 1024), T.pu[:, 1024 * j:1024 * j + 1024], "lpu%d" % j)

    def col(j):
        return A("PF", j, j + 1)

    CK = [[0, 16], [1, 16]]
    iota(A("PI", 0, 1), [[0, 1]], 0, 1)
    iota(A("IF"), [[1, 144]], 0, 0)
    iota(A("ONB"), [[0, 128]], 1, 0)
    keep(A("ID"), A("ONB"), [[-1, 128]], OP.is_equal, 0.0, 0, 1)
    act(A("NID"), A("ID"), scale=-1.0)
    iota(A("KREV"), [[0, 16], [-1, 16]], 15, 0)
    keep(A("KRV0"), A("KREV", 0, 128), [[0, 8], [1, 16]], OP.is_gt, -BIG, 0, 0)
    iota(A("ONF"), [[0, 256]], 1, 0)
    keep(A("RES1"), A("ONF"), CK, OP.is_equal, 0.0, 0, 0)
    iota(A("NEGC"), [[0, 128]], -262144, 0)
    keep(A("NEGM"), A("NEGC"), [[0, 8], [-1, 16]], OP.is_ge, 0.0, 14, 0)
    keep(A("RES"), A("ONF"), CK, OP.is_gt, 0.0, 0, 0)
    for r in range(NR):
        iota(A("PA0" if r == 0 else "PAS%d" % r, 0, 1), [[0, 1]], 1, 0)
    iota(A("MU"), [[0, 8], [1, 16]], 0, 0)
    iota(A("MG"), [[1, 8], [0, 16]], 0, 0)
    iota(A("IV"), [[1, 128]], 0, 0)
    iota(A("KFW"), [[0, 8], [1, 16]], 0, 0)
    iota(A("BASE"), [[16, 16]], 2048, 0)
    iota(A("BKA"), [[0, 256]], 0, 0)
    iota(A("BKB"), [[0, 256]], 0, 0)
    iota(A("BGC"), [[0, 16], [-1, 16]], 262144 + 15, 0)
    keep(A("BIGK"), A("BGC"), CK, OP.is_gt, 0.0, 0, 0)
    AND, SHR = OP.bitwise_and, OP.arith_shift_right
    ts(A("PI", 1, 2), A("PI", 0, 1), 15, AND)
    ts(A("PI", 2, 3), A("PI", 0, 1), 4, SHR)
    ts(A("PI", 3, 4), A("PI", 0, 1), 4, SHR, 1, AND)
    ts(A("PI", 4, 5), A("PI", 0, 1), 112, AND)
    cp(A("PF", 0, 5), A("PI", 0, 5))
    ts(A("PF", 6, 7), A("PF", 3, 4), -1000.0, OP.mult)
    ts(A("PF", 7, 8), A("PF", 3, 4), 1000.0, OP.mult, -1000.0, OP.add)
    tt(A("PF", 8, 9), A("PF", 6, 7), A("PF", 0, 1), OP.add)
    tt(A("PF", 9, 10), A("PF", 7, 8), A("PF", 0, 1), OP.add)
    ts(A("PF", 10, 11), A("PF", 4, 5), 15.0, OP.add)
    for x in range(2):
        for y in range(2):
            j = 2 * x + y
            ts(A("SW", 128 * j, 128 * j + 128), A("IF", 0, 128), float(16 * (y - x)), OP.subtract, col(8 + x), OP.is_equal)

    def swap(dst, src):
        for x in range(2):
            for y in range(2):
                j = 2 * x + y
                mm(B(T[dst][:, x:16:2, :], dst, 0, 16), A("SW", 128 * j, 128 * j + 128), B(T[src][:, y:16:2, :], src, 0, 16), y == 0, y == 1)

    def offs(o):
        for h in range(4):
            ts(A(o, 64 * h, 64 * h + 64), A("PFL", h, 256, 4), 2048.0, OP.mult)

    def spread(yn, c0, c1, q):
        f = cp if q == "V" else (lambda o, i: act(o, i, AF.Copy))
        X, y = T.XQ, A(yn, 16 * c0, 16 * c1)
        f(B(X[:, c0:c1, 0, :], "XQ", 4 * c0, 4 * c0 + 1), y)
        f(B(X[:, c0:c1, 1, :], "XQ", 4 * c0 + 1, 4 * c0 + 2), y)
        f(B(X[:, c0:c1, 2:4, :], "XQ", 4 * c0 + 2, 4 * c0 + 4), B(X[:, c0:c1, 0:2, :], "XQ", 4 * c0, 4 * c0 + 2))
        f(A("XR", 64 * c0, 64 * c1), B(X[:, c0:c1, :, :], "XQ", 4 * c0, 4 * c0 + 4))

    for h in range(2):
        ts(A("Y0", 128 * h, 128 * h + 128), A("X0R", h, 256, 2), -1.0, OP.mult, 256.0, OP.add)
    spread("Y0", 0, 8, "V")
    spread("Y0", 8, 16, "S")
    for h in range(2):
        cp(A("A16", 128 * h, 128 * h + 128), A("P0R", h, 256, 2))
    t32(A("C16"), A("A16"))
    swap("sps", "C16")
    SD = B(T.sps[:, 0:16, :], "sps", 0, 16)
    ts(A("PFL"), SD, 2.0 ** -11, OP.mult)
    offs("PO0")
    ts(A("FS"), A("IF"), col(10), OP.is_equal, 32.0, OP.mult)

    def pay0():
        act(A("TA"), A("PFL"), bias=1.0)
        act(A("TB"), A("PFL"), scale=2.0 ** -11)

    def pay1(pa):
        tt(A(pa, 1, 256), A("TA", 1, 256), A("TB", 0, 255), OP.add)

    def pens(km):
        tt(A("EQ"), A("PFL", 0, 128), A("PFL", 128, 256), OP.is_equal)
        scan(A("PRE"), A("RES1", 0, 128), A("EQ"), OP.max, OP.min)
        tt(A("PM"), A("PRE"), A("NEGM"), OP.mult)
        tt(A(km), A("PM"), A("KRV0"), OP.add)

    for j in range(4):
        o, i = A("TX", 512 * j, 512 * j + 512), A("TXR", 512 * j, 512 * j + 512)
        if j % 2 == 0:
            ts(o, i, -1.0, OP.mult, 256.0, OP.add)
        else:
            act(o, i, scale=-1.0, bias=256.0)
    WIN = A("TX", 0, 2048)

    def tables():
        ts(A("BDM"), A("MG"), col(2), OP.is_equal)
        ts(A("T1", 0, 128), A("MU"), 1.0, OP.add)
        tt(A("T1", 128, 256), A("T1", 0, 128), A("BDM"), OP.mult)
        ts(A("IU"), A("T1", 128, 256), -1.0, OP.add)

    def tables2():
        ts(A("BD"), A("BDM"), -256.0, OP.mult)
        ts(A("H16"), A("IF", 0, 16), col(1), OP.is_equal)
        for u in range(16):
            ts(A("REP", 128 * u, 128 * u + 128), A("BD"), A("H16", u, u + 1), OP.mult)
        ts(A("O1"), A("BASE"), col(1), OP.add)
        ts(A("BASE"), A("O1"), 2.0 ** -11, OP.mult)

    def dist(off, ps, ex, hooks=()):
        do("S", lambda: g.scalar.activation(T.TG[:], T.TX[:, 0:2048].indirect(T[off][:, 32:64]), AF.Copy, bias=0.0, scale=1.0),
           [A("TG")], [WIN, A(off, 32, 64)])
        mm(A("t3"), A("ID"), A("TG"), True, False)
        mm(A("t3"), A("NID"), A("XR", 512, 1024), False, True)
        for h in range(4):
            lo, hi = 1024 * h, 1024 * h + 1024
            m = hi if h else lo + 512
            gat(A("DF", lo, m), WIN, A(off, lo // 16, m // 16), A("XR", 0, m - lo), OP.subtract)
            if h < len(hooks):
                hooks[h]()
            out = A(ps, h, 256, 4)
            st = (1, 2, 2, 4)[h]
            n = 0
            for b0 in range(st):
                nm = "AD%d_%d" % (h, b0)
                act(B(T.AD[:, lo + b0:m:st], nm, lo, m), B(T.DF[:, lo + b0:m:st], "DF", lo, m), AF.Abs)
                if h == 0:
                    act(B(T.AD[:, m:hi], nm, m, hi), A("t3"), AF.Abs)
                for b in range(b0, 16, st):
                    mm(out, A("FS", 15 - b, 143 - b), B(T.AD[:, lo + b:hi:16], nm, lo, hi), n == 0, n == 15)
                    n += 1
                    if n == (4 if h == 3 else 14):
                        for c in (0, 128):
                            mm(A(ps, c + h, c + 128, 4), A("ID"), A(ex, h, 128, 4), False, False)

    def latch(key, pay, res, o0, o1):
        scan(A("FM"), A(res), key, o0, o1)
        tt(A("RR"), key, A("FM"), OP.is_equal)
        tt(A("D1"), pay, A("RR"), OP.subtract)
        scan(A("LT"), A("RR"), A("D1"), OP.max, OP.min)

    LAST = A("LT", 15, 256, 16)
    FML = A("FM", 15, 256, 16)
    DPS, EPS = A("dps", 0, 256), A("eps", 0, 256)
    PAE = A("kps", 128, 384)
    PAP = A("t2", 0, 256)
    BGP = A("eps", 256, 512)
    MPS = A("dps", 256, 384)
    OH = A("dps", 256, 512)
    PX = A("t0", 0, 256)
    for r in range(NR):
        last = r == NR - 1
        Y, PO, KM, PA, MK, MS = ["%s%d" % (n, r) for n in ("Y", "PO", "KM", "PA", "MK", "MS")]
        if r:
            for n, s in ((Y, "ry"), (PO, "rp"), (KM, "rk"), (PA, "ra")):
                land(A(n), "%s_%d" % (s, r), prv, [core])
        if r:
            spread(Y, 0, 8, "V")
            spread(Y, 8, 16, "S")
        else:
            pay0()
        dist(PO, "dps", KM, (lambda: pens("KM0"), tables, lambda: pay1("PA0")) if r == 0 else ())
        act(A("TX", 2048, 2304), A(Y), AF.Copy)
        act(PAP, A(PA), AF.Copy)
        if r == 0:
            act(A("RESB"), A("RES1"), scale=1048576.0)
            act(BGP, A("BIGK"), AF.Copy)
        else:
            act(A("THA"), A(KM), AF.Relu, scale=-1.0)
            for h in range(2):
                act(A("THB", 128 * h, 128 * h + 128), A("THA"), scale=-1.0, bias=65536.0)
        latch(DPS, PAP, "RES", OP.mult, OP.max)
        ts(A("PAYI"), LAST, 4194304.0, OP.mult)
        ts(A("UVI", 0, 16), A("PAYI"), 18, SHR)
        ts(A("UVI", 16, 32), A("PAYI"), 11, SHR, 127, AND)
        cp(A("UVF"), A("UVI"))
        for c in range(16):
            lo, hi = 128 * c, 128 * c + 128
            ts(A("OU", lo, hi), A("IU"), A("UVF", c, c + 1), OP.is_equal)
            ts(A("OV", lo, hi), A("IV"), A("UVF", 16 + c, 17 + c), OP.is_equal)
            mm(MPS, A("OU", lo, hi), A("OV", lo, hi), c == 0, c == 15)
        ts(A(MS), MPS, 0.5, OP.is_ge)
        send(A(MS), rest(rank), T[MK][:, 128 * rank:128 * rank + 128], "mk%d_%d" % (r, rank))
        for j in range(NG):
            if j != rank:
                land(A(MK, 128 * j, 128 * j + 128), "mk%d_%d" % (r, j), T.cores[j], rest(j))
        if r:
            tt(A("T1"), DPS, A("THB"), OP.is_ge)
            tt(A("D1"), A("T1"), BGP, OP.mult)
            tt(DPS, DPS, A("D1"), OP.max)
            latch(DPS, PAP, "RES", OP.mult, OP.max)
            ts(A("PAYI"), LAST, 4194304.0, OP.mult)
        ts(A("TEI"), A("PAYI"), 2047, AND)
        cp(A("TEO"), A("TEI"))
        gat(A("A16"), A("PU"), A("TEO"))
        t32(A("C16"), A("A16"))
        swap("sps", "C16")
        cp(A("DKI"), FML)
        ts(A("PKI"), A("PAYI"), 11, SHR)
        ts(A("DKJ"), A("DKI"), 15, AND)
        ts(A("PK"), A("PKI"), 2.0 ** -11, OP.mult)
        ts(A("DKM"), FML, 16.0, OP.subtract, 65536.0, OP.min)
        cp(A("BKA", 0, 256, 16), A("DKJ"))
        if r == 0:
            tables2()
        else:
            for h in range(4):
                ts(A("PFL", h, 256, 4), A(PO, 64 * h, 64 * h + 64), 2.0 ** -11, OP.mult)
        scan(OH, A("RES"), A("BKA"), OP.mult, OP.add)
        def bank(q, lo, hi):
            return A("t%d" % q, lo, hi)
        order = (3, 0, 2, 1)
        for q in order:
            mm(bank(q, 0, 512), A("ID"), A("TX", 512 * q, 512 * q + 512), True, False)
        mm(A("kps", 0, 128), A("ID"), A(MS), True, False)
        js = [j for j in range(NG) if j != rank]
        for j in js:
            mm(A("kps", 0, 128), A("ID"), A(MK, 128 * j, 128 * j + 128), False, j == js[-1])
        ts(A("CUT"), A("kps", 0, 128), 3.5, OP.is_ge)
        for q in order:
            for u in range(4):
                v = 4 * q + u
                mm(bank(q, 128 * u, 128 * u + 128), A("REP", 128 * v, 128 * v + 128), A("CUT"), False, u == 3)
        for h in range(4):
            cp(A("PDO", 64 * h, 64 * h + 64), B(T.sps[:, 0:16, h:16:4], "sps", 0, 16))
        for n, q in enumerate(order):
            o = A("TX", 512 * q, 512 * q + 512)
            if n % 2 == 0:
                ts(o, bank(q, 0, 512), 0.0, OP.max)
                if n == 0:
                    tt(OH, OH, A("KREV"), OP.is_equal)
            else:
                act(o, bank(q, 0, 512), AF.Relu)
        dist("PDO", "eps", "KFW")
        if r == 0:
            cp(A("CAC"), A("CUT"))
        else:
            tt(A("CA2" if r == 1 else "CAC"), A("CAC" if r == 1 else "CA2"), A("CUT"), OP.max)
        ts(PAE, SD, 2.0 ** -11, OP.mult, 1.0, OP.add)
        tt(PX, OH, A("PFL"), OP.mult)
        tt(A("PZ"), A("PFL"), PX, OP.subtract)
        latch(EPS, PAE, "RESB", OP.add, OP.min)
        tt(A("O1"), LAST, A("BASE"), OP.subtract)
        tt(A("TK"), A("DKM"), FML, OP.is_ge)
        tt(A("N1"), LAST, A("PK"), OP.subtract)
        tt(A("O2"), A("O1"), A("TK"), OP.mult)
        tt(A("N2"), A("N1"), A("TK"), OP.mult)
        tt(A("OF"), A("O2"), A("BASE"), OP.add)
        tt(A("BKB", 0, 256, 16), A("N2"), A("PK"), OP.add)
        ts(A("OFO"), A("OF"), 2048.0, OP.mult)
        gat(A("SU"), A("TX"), A("OFO"), A(Y), OP.add)
        e = r + 1
        YS = "YS%d" % e
        act(A(YS), A("SU"), scale=0.5, bias=0.25)
        if not last:
            send(A(YS), [nxt], T["Y%d" % e][:], "ry_%d" % e)
        NB, NV = A("T1"), A("t0", 256, 512)
        scan(NB, A("RES"), A("BKB"), OP.mult, OP.add)
        tt(NV, OH, NB, OP.mult)
        if not last:
            tt(A("PFL"), A("PZ"), NV, OP.add)
            offs("POS%d" % e)
            send(A("POS%d" % e), [nxt], T["PO%d" % e][:], "rp_%d" % e)
            pay0()
            pens("KMS%d" % e)
            pay1("PAS%d" % e)
            send(A("KMS%d" % e), [nxt], T["KM%d" % e][:], "rk_%d" % e)
            send(A("PAS%d" % e), [nxt], T["PA%d" % e][:], "ra_%d" % e)
        else:
            tt(A("PNH"), A("PZ"), NV, OP.add)
            swap("sps", "PNH")
            for h in range(2):
                act(A("YXB", h, 256, 2), A(YS, 128 * h, 128 * h + 128), scale=-1.0, bias=256.0)
            store("Y", T.yx[:], A("YXB"), "oyx")
            store("Y", T.yc[:], A("CAC"), "oyc")
            t32(A("YPA"), SD)
            ts(A("YPB", 0, 256, 2), A("YPA", 0, 128), 2048.0, OP.mult)
            act(A("YPB", 1, 256, 2), A("YPA", 128, 256), scale=2048.0)
            store("Y", T.yp[:], A("YPB"), "oyp")

    for s in ["oyp", "oyx", "oyc"] + LOADS:
        g.sync.wait_ge(T.sem[s], 16)
    g.wait_ge(T.sem.loc, sent[0])
    for q in ("V", "S", "P", "G"):
        g.wait_ge(T.sem[SEM[q]], cnt[q])
